import numpy as np
import ml_dtypes


def mxq(x, axis, fmt="e4m3"):
    dtype, down = {"e4m3": (ml_dtypes.float8_e4m3fn, 7), "e5m2": (ml_dtypes.float8_e5m2, 14)}[fmt]
    v = np.moveaxis(np.asarray(x, np.float32).astype(ml_dtypes.bfloat16).astype(np.float64), axis, -1)
    blocks = v.reshape(v.shape[:-1] + (-1, 32))
    amax = np.abs(blocks).max(-1, keepdims=True)
    byte = np.maximum(np.where(amax > 0, np.frexp(amax)[1] - 1 + 127, 0) - down, 1)
    scale = np.exp2(byte - 127.0)
    codes = (blocks / scale).astype(np.float32).astype(dtype).astype(np.float64)
    return np.moveaxis((codes * scale).reshape(v.shape), -1, axis)


WIDE = False


def mx_kscale(k):
    if not WIDE:
        return np.ones(k)
    levels = np.array([10, -10, 5, -5, 0])
    if k % 512:
        return np.exp2(np.random.permutation(np.resize(levels, k // 32))).repeat(32)
    a = np.empty((k // 512, 16))
    for p in range(k // 512):
        a[p, :8] = np.random.permutation(np.resize(levels, 8))
        for g in range(8):
            far = levels[np.abs(levels - a[p, g]) >= 10]
            a[p, g + 8] = far[np.random.randint(len(far))]
    return np.exp2(a.ravel()).repeat(32)


def f64(x):
    return np.asarray(x).astype(np.float64)


def striped(idx):
    return np.tile(idx.reshape(-1, 16).T, (8, 1)).astype(np.uint16)


def unstriped(offs):
    return offs[:16].T.reshape(-1).astype(np.int64)


E2M1 = np.array([0.0, 0.5, 1.0, 1.5, 2.0, 3.0, 4.0, 6.0, -0.0, -0.5, -1.0, -1.5, -2.0, -3.0, -4.0, -6.0])


def pack_weight(w, fmt):
    k, n = w.shape
    w = f64(np.asarray(w, np.float32).astype(ml_dtypes.bfloat16)).reshape(k // 32, 32, n)
    amax = np.abs(w).max(1)
    if fmt == "e4m3":
        byte = np.frexp(amax)[1] - 1 + 127 - 7
    else:
        mant, ex = np.frexp(amax / 6.0)
        byte = np.where(mant > 0.5, ex, ex - 1) + 127
    byte = np.clip(np.where(amax > 0, byte, 1), 1, 254)
    scaled = (w * np.exp2(127.0 - byte)[:, None, :]).reshape(k, n).astype(np.float32)
    by_word = np.ascontiguousarray(scaled.reshape(k // 512, 128, 4, n).transpose(0, 1, 3, 2))
    if fmt == "e4m3":
        words = by_word.astype(ml_dtypes.float8_e4m3fn).view(np.uint8)
    else:
        c = by_word.astype(ml_dtypes.float4_e2m1fn).view(np.uint8) & 0xF
        words = (c[..., 0::2] | (c[..., 1::2] << 4)).reshape(k // 512, 128, 2 * n)
    return np.ascontiguousarray(words), np.ascontiguousarray(byte.astype(np.uint8).reshape(k // 512, 16, n))


def unpack_weight(words, scales, fmt):
    g, _, n = scales.shape
    words = np.ascontiguousarray(words).reshape(g, 128, n, -1)
    if fmt == "e4m3":
        vals = words.view(ml_dtypes.float8_e4m3fn).astype(np.float64)
    else:
        nib = np.empty((g, 128, n, 4), np.uint8)
        nib[..., 0::2] = words & 0xF
        nib[..., 1::2] = words >> 4
        vals = E2M1[nib]
    vals = vals * np.repeat(np.exp2(scales.astype(np.float64) - 127.0), 8, axis=1)[..., None]
    return vals.transpose(0, 1, 3, 2).reshape(g * 512, n)


def gelu(v):
    return 0.5 * v * (1.0 + np.tanh(np.sqrt(2.0 / np.pi) * (v + 0.044715 * v**3)))


K, H, N, T, S = 1024, 1024, 384, 4096, 1024

def setup_inputs():
    n = np.random.standard_normal
    s = mx_kscale(K)[:, None]
    u = mx_kscale(H)[:, None]
    tab_words, tab_scales = pack_weight(n((K, T)) * s, "e2m1")
    wx_words, wx_scales = pack_weight(1.5 * n((K, H)) / np.sqrt(K) / s, "e4m3")
    w4_words, w4_scales = pack_weight(n((H, N)) / np.sqrt(H) / u, "e2m1")
    return {
        "tab_words": tab_words, "tab_scales": tab_scales,
        "offs": striped(np.random.permutation(T)[:S]),
        "offs2": striped(np.random.permutation(T)[:S]),
        "we": (1.5 * n((K, H)) / np.sqrt(K) / s).astype(np.float32),
        "wx_words": wx_words, "wx_scales": wx_scales,
        "sat": (0.5 + 0.5 * n(H)).astype(np.float32),
        "gain": (np.exp(0.3 * n(H)) * u[:, 0]).astype(np.float32),
        "w4_words": w4_words, "w4_scales": w4_scales,
    }

def reference(tab_words, tab_scales, offs, offs2, we, wx_words, wx_scales, sat, gain, w4_words, w4_scales):
    TW = unpack_weight(tab_words, tab_scales, "e2m1")
    v = TW[:, unstriped(offs)]
    v2 = TW[:, unstriped(offs2)]
    wx = unpack_weight(wx_words, wx_scales, "e4m3")
    w4 = unpack_weight(w4_words, w4_scales, "e2m1")
    e = mxq(f64(we), 0, "e4m3").T @ v
    x = wx.T @ v2
    d = np.maximum(e, x) - f64(sat)[:, None]
    h = np.sqrt(np.square(d) + 1.0) * f64(gain)[:, None]
    return w4.T @ mxq(h, 0, "e4m3")

@@ -1,0 +1,290 @@
+from contextlib import ExitStack
+
+import concourse.mybir as mybir
+
+K, H, N, T, S = 1024, 1024, 384, 4096, 1024
+FLOPS = 2 * (2 * K * H * S + H * N * S)
+
+F32 = mybir.dt.float32
+BF16 = mybir.dt.bfloat16
+I32 = mybir.dt.int32
+U16 = mybir.dt.uint16
+U8 = mybir.dt.uint8
+FP8X4 = mybir.dt.float8_e4m3fn_x4
+FP4X4 = mybir.dt.float4_e2m1fn_x4
+ALU = mybir.AluOpType
+ACT = mybir.ActivationFunctionType
+
+P = 128
+PACK = 4
+PASS = P * PACK
+PASSES = 2
+HALF = 512
+HALVES = S // HALF
+QUADS = 4
+ENTRY, EXIT = 0, 1
+CHUNK = 128
+
+
+def tile_list_junction_turn_delay_kernel(
+    tc, tab_words, tab_scales, offs, offs2, we, wx_words, wx_scales, sat, gain, w4_words, w4_scales, out
+):
+    nc = tc.nc
+    with ExitStack() as ctx:
+        keep = ctx.enter_context(tc.tile_pool(name="keep", bufs=1))
+        work = ctx.enter_context(tc.tile_pool(name="work", bufs=2))
+        shared = ctx.enter_context(tc.tile_pool(name="shared", bufs=1))
+        psum = ctx.enter_context(tc.psum_pool(name="psum", bufs=1))
+
+        def held(name, shape, dtype, offset=None):
+            if offset is None:
+                return keep.tile(shape, dtype, name=name, align_bytes=64)
+            return shared.tile(shape, dtype, name=name, align_bytes=64, offset=offset)
+
+        lists = [held("entry_list", [P, S // 16], U16), held("exit_list", [P, S // 16], U16)]
+        table_scales = held("table_scales", [P, T], U8)
+        table_words = [held(f"table_words{a}", [P, T], U16) for a in range(PASSES)]
+        wx_raw = [held(f"wx_raw{b}", [P, PASSES, PASS], I32) for b in range(PASSES)]
+        wx_scale_raw = held("wx_scale_raw", [P, PASSES, H], U8)
+        we_raw = [[held(f"we_raw{b}{a}", [P, PACK, PASS], F32) for a in range(PASSES)] for b in range(PASSES)]
+        w4_codes = held("w4_codes", [P, PASSES * 2 * N], U8)
+        w4_plane = held("w4_plane", [P, PASSES * N], U8)
+        sat_cols = held("sat_cols", [P, PASSES, PACK], F32)
+        neg_sat = held("neg_sat", [P, PASSES, PACK], F32)
+        gain_cols = held("gain_cols", [P, PASSES, PACK], F32)
+        second_plane = [[held(f"second_plane{s}{h}", [P, HALF], U8) for h in range(HALVES)] for s in (ENTRY, EXIT)]
+        warm = held("warm", [P, 2], F32)
+
+        nc.vector.memset(table_scales[:, : 3 * T // 4].bitcast(I32), 0)
+        nc.gpsimd.memset(table_scales[:, 3 * T // 4 :].bitcast(I32), 0)
+        nc.vector.memset(wx_scale_raw[:].bitcast(I32), 0)
+        for h in range(HALVES):
+            for s in (EXIT, ENTRY):
+                nc.vector.memset(second_plane[s][h][:].bitcast(I32), 0)
+        nc.vector.memset(w4_plane[:].bitcast(I32), 0)
+        nc.vector.memset(warm[:, 0:1], 1.0)
+        nc.scalar.activation(warm[:, 1:2], warm[:, 0:1], ACT.Sqrt)
+
+        def load_we(b, a):
+            rows = we[a * PASS : (a + 1) * PASS, b * PASS : (b + 1) * PASS]
+            nc.sync.dma_start(out=we_raw[b][a][:], in_=rows.rearrange("(p i) c -> p i c", i=PACK))
+
+        def load_wx(b):
+            words = wx_words.rearrange("a p c i -> p a (c i)")[:, :, b * PASS * PACK : (b + 1) * PASS * PACK]
+            nc.sync.dma_start(out=wx_raw[b][:], in_=words.bitcast(I32))
+
+        nc.sync.dma_start(lists[EXIT][:], offs2)
+        nc.sync.dma_start(lists[ENTRY][:], offs)
+        for r in range(4):
+            nc.scalar.dma_start(
+                out=table_scales[r:P:16, :].bitcast(I32),
+                in_=tab_scales.rearrange("a (q r) c -> r q a c", r=4)[r].bitcast(I32),
+            )
+        for a in range(PASSES):
+            nc.sync.dma_start(out=table_words[a][:].bitcast(I32), in_=tab_words[a].bitcast(I32))
+        for q in range(QUADS):
+            nc.gpsimd.dma_start(
+                out=wx_scale_raw[32 * q : 32 * q + 4, :, :].bitcast(I32),
+                in_=wx_scales[:, 4 * q : 4 * q + 4, :].rearrange("a r c -> r a c").bitcast(I32),
+            )
+        nc.gpsimd.dma_start(out=sat_cols[:], in_=sat.rearrange("(b p t) -> p b t", b=PASSES, t=PACK))
+        nc.gpsimd.tensor_scalar(neg_sat[:], sat_cols[:], -1.0, 0.0, ALU.mult, ALU.add)
+        load_wx(0)
+        load_we(0, 0)
+        load_we(0, 1)
+        load_wx(1)
+        load_we(1, 0)
+        load_we(1, 1)
+
+        picked_words = {}
+        first_plane = {}
+
+        def gather_scales(s, h, offset=None):
+            cols = lists[s][:, h * HALF // 16 : (h + 1) * HALF // 16]
+            both = held(f"picked_scales{s}{h}", [P, HALF], U8, offset)
+            nc.vector.tensor_copy(both[:], table_scales[:].indirect(cols))
+            first_plane[s, h] = both
+            queue = nc.scalar if h == 0 else nc.sync
+            queue.dma_start(out=second_plane[s][h][0:100, :].bitcast(I32), in_=both[16:116, :].bitcast(I32))
+
+        def gather_words(s, h, a, offset=None):
+            cols = lists[s][:, h * HALF // 16 : (h + 1) * HALF // 16]
+            words = held(f"picked_words{s}{h}{a}", [P, HALF], U16, offset)
+            nc.vector.tensor_copy(words[:], table_words[a][:].indirect(cols))
+            picked_words[s, h, a] = words
+
+        codes = {}
+        planes = {}
+
+        def order_wx(b):
+            words = held(f"wx_codes{b}", [P, PASSES, PASS], I32)
+            nc.vector.tensor_copy(
+                words[:].rearrange("p a (t g m) -> p a g t m", t=PACK, m=4),
+                wx_raw[b][:].rearrange("p a (g m t) -> p a g t m", t=PACK, m=4),
+            )
+            plane = held(f"wx_plane{b}", [P, PASSES, PASS], U8)
+            nc.vector.tensor_copy(
+                plane[:].rearrange("p a (t m) -> p a t m", t=PACK),
+                wx_scale_raw[:, :, b * PASS : (b + 1) * PASS].rearrange("p a (m t) -> p a t m", t=PACK),
+            )
+            for a in range(PASSES):
+                codes[EXIT, b, a] = words[:, a, :]
+                planes[EXIT, b, a] = plane[:, a, :]
+
+        rounded_we = {}
+
+        def round_we(b, a, copy):
+            rounded = held(f"we_rounded{b}{a}", [P, PASS * PACK], BF16, 4096 * (2 * b + a))
+            copy(
+                rounded[:].rearrange("p (t m i) -> p m i t", t=PACK, i=PACK),
+                we_raw[b][a][:].rearrange("p i (m t) -> p m i t", t=PACK),
+            )
+            rounded_we[b, a] = rounded
+
+        def quantize_we(b, a):
+            words = held(f"we_codes{b}{a}", [P, PASS], I32)
+            plane = held(f"we_plane{b}{a}", [P, PASS], U8)
+            nc.vector.quantize_mx(out=words[:].bitcast(FP8X4), scales=plane[:], in_=rounded_we[b, a][:])
+            codes[ENTRY, b, a] = words[:]
+            planes[ENTRY, b, a] = plane[:]
+
+        def response(s, h, b, t, bank):
+            cols = slice(t * P, (t + 1) * P)
+            for a in range(PASSES):
+                nc.tensor.matmul_mx(
+                    out=bank[:],
+                    lhsT=codes[s, b, a][:, cols].bitcast(FP8X4),
+                    lhsT_scale=planes[s, b, a][:, cols],
+                    rhs=picked_words[s, h, a][:].bitcast(FP4X4),
+                    rhs_scale=(first_plane[s, h] if a == 0 else second_plane[s][h])[:],
+                    start=(a == 0),
+                    stop=(a == PASSES - 1),
+                )
+
+        exit_less_sat = {}
+
+        def exit_response(h, b):
+            shifted = held(f"exit_less_sat{h}{b}", [P, PACK, HALF], F32)
+            for t in range(PACK):
+                bank = psum.tile([P, HALF], F32, name="exit_bank", tag="exit_bank", bufs=2)
+                response(EXIT, h, b, t, bank)
+                nc.scalar.activation(shifted[:, t, :], bank[:], ACT.Identity, bias=neg_sat[:, b, t : t + 1])
+            exit_less_sat[h, b] = shifted
+
+        roots = {}
+
+        def smooth(h, b):
+            larger = work.tile([P, PACK, HALF], F32, name="larger")
+            squared = work.tile([P, PACK, HALF], F32, name="squared")
+            root = work.tile([P, PACK, HALF], F32, name="root")
+            for t in range(PACK):
+                bank = psum.tile([P, HALF], F32, name="entry_bank", tag="entry_bank", bufs=3)
+                response(ENTRY, h, b, t, bank)
+                nc.vector.scalar_tensor_tensor(
+                    larger[:, t, :], bank[:], sat_cols[:, b, t : t + 1], exit_less_sat[h, b][:, t, :],
+                    ALU.subtract, ALU.max,
+                )
+                nc.scalar.activation(squared[:, t, :], larger[:, t, :], ACT.Square)
+                nc.scalar.activation(root[:, t, :], squared[:, t, :], ACT.Sqrt, bias=1.0)
+            roots[h, b] = root
+
+        h_codes = {}
+        h_planes = {}
+
+        def quantize_h(h, b, width):
+            words = held(f"h_codes{h}{b}", [P, HALF], I32)
+            plane = held(f"h_plane{h}{b}", [P, HALF], U8)
+            rounded = held(f"h_rounded{h}{b}", [P, HALF * PACK], BF16)
+            for c0 in range(0, HALF, width):
+                part = rounded[:, c0 * PACK : (c0 + width) * PACK]
+                nc.vector.tensor_tensor(
+                    part.rearrange("p (c j t) -> p c t j", t=PACK, j=4),
+                    roots[h, b][:, :, c0 : c0 + width].rearrange("p t (c j) -> p c t j", j=4),
+                    gain_cols[:, b, :].unsqueeze(1).unsqueeze(3).to_broadcast([P, width // 4, PACK, 4]),
+                    ALU.mult,
+                )
+            for c0 in range(0, HALF, width):
+                nc.vector.quantize_mx(
+                    out=words[:, c0 : c0 + width].bitcast(FP8X4),
+                    scales=plane[:, c0 : c0 + width],
+                    in_=rounded[:, c0 * PACK : (c0 + width) * PACK],
+                )
+            h_codes[h, b] = words
+            h_planes[h, b] = plane
+
+        def project(h, n, c0, width, dest):
+            for b in range(PASSES):
+                nc.tensor.matmul_mx(
+                    out=dest,
+                    lhsT=w4_codes[:, 2 * (b * N + n * P) : 2 * (b * N + (n + 1) * P)].bitcast(FP4X4),
+                    lhsT_scale=w4_plane[:, b * N + n * P : b * N + (n + 1) * P],
+                    rhs=h_codes[h, b][:, c0 : c0 + width].bitcast(FP8X4),
+                    rhs_scale=h_planes[h, b][:, c0 : c0 + width],
+                    start=(b == 0),
+                    stop=(b == PASSES - 1),
+                )
+
+        def project_wide(h):
+            for n in range(N // P):
+                bank = psum.tile([P, HALF], F32, name="out_bank", tag="out_bank", bufs=3)
+                project(h, n, 0, HALF, bank[:])
+                staged = held(f"staged{h}{n}", [P, HALF], F32)
+                nc.scalar.copy(staged[:], bank[:])
+                nc.sync.dma_start(out=out[n * P : (n + 1) * P, h * HALF : (h + 1) * HALF], in_=staged[:])
+
+        def project_narrow(h):
+            for c0 in range(0, HALF, CHUNK):
+                bank = psum.tile([P, N // P, CHUNK], F32, name="out_bank_narrow", tag="out_bank", bufs=3)
+                for n in range(N // P):
+                    project(h, n, c0, CHUNK, bank[:, n, :])
+                staged = held(f"staged_narrow{c0}", [P, N // P, CHUNK], F32)
+                nc.scalar.copy(staged[:], bank[:])
+                cols = out[:, h * HALF + c0 : h * HALF + c0 + CHUNK]
+                nc.sync.dma_start(out=cols.rearrange("(n p) c -> p n c", p=P), in_=staged[:])
+
+        gather_scales(EXIT, 0)
+        gather_scales(ENTRY, 0)
+        gather_words(EXIT, 0, 0)
+        gather_words(ENTRY, 0, 0)
+        gather_words(EXIT, 0, 1)
+        order_wx(0)
+        gather_words(ENTRY, 0, 1)
+        exit_response(0, 0)
+        round_we(0, 0, nc.scalar.copy)
+        round_we(0, 1, nc.vector.tensor_copy)
+        quantize_we(0, 0)
+        quantize_we(0, 1)
+        nc.gpsimd.dma_start(out=gain_cols[:], in_=gain.rearrange("(b p t) -> p b t", b=PASSES, t=PACK))
+        nc.gpsimd.dma_start(
+            out=w4_codes[:].rearrange("p (a c) -> p a c", a=PASSES).bitcast(I32),
+            in_=w4_words.rearrange("a p c -> p a c").bitcast(I32),
+        )
+        for q in range(QUADS):
+            nc.gpsimd.dma_start(
+                out=w4_plane[32 * q : 32 * q + 4, :].rearrange("p (a c) -> p a c", a=PASSES).bitcast(I32),
+                in_=w4_scales[:, 4 * q : 4 * q + 4, :].rearrange("a r c -> r a c").bitcast(I32),
+            )
+        order_wx(1)
+        smooth(0, 0)
+        gather_scales(EXIT, 1, 4096 + 2048)
+        gather_words(EXIT, 1, 0, 4096)
+        gather_words(EXIT, 1, 1, 4096 + 1024)
+        exit_response(0, 1)
+        round_we(1, 0, nc.scalar.copy)
+        round_we(1, 1, nc.vector.tensor_copy)
+        quantize_we(1, 0)
+        quantize_we(1, 1)
+        gather_scales(ENTRY, 1, 3 * 4096 + 2048)
+        gather_words(ENTRY, 1, 0, 3 * 4096)
+        gather_words(ENTRY, 1, 1, 3 * 4096 + 1024)
+        smooth(0, 1)
+        quantize_h(0, 0, 512)
+        exit_response(1, 0)
+        smooth(1, 0)
+        quantize_h(0, 1, 512)
+        project_wide(0)
+        exit_response(1, 1)
+        smooth(1, 1)
+        quantize_h(1, 0, 512)
+        quantize_h(1, 1, CHUNK)
+        project_narrow(1)

@@ -52,15 +52,14 @@ def tile_list_junction_turn_delay_kernel(
         sat_cols = held("sat_cols", [P, PASSES, PACK], F32)
         neg_sat = held("neg_sat", [P, PASSES, PACK], F32)
         gain_cols = held("gain_cols", [P, PASSES, PACK], F32)
-        second_plane = [[held(f"second_plane{s}{h}", [P, HALF], U8) for h in range(HALVES)] for s in (ENTRY, EXIT)]
+        second_plane = [held(f"second_plane{h}", [P, 2 * HALF], U8) for h in range(HALVES)]
         warm = held("warm", [P, 2], F32)
 
         nc.vector.memset(table_scales[:, : 3 * T // 4].bitcast(I32), 0)
         nc.gpsimd.memset(table_scales[:, 3 * T // 4 :].bitcast(I32), 0)
         nc.vector.memset(wx_scale_raw[:].bitcast(I32), 0)
         for h in range(HALVES):
-            for s in (EXIT, ENTRY):
-                nc.vector.memset(second_plane[s][h][:].bitcast(I32), 0)
+            nc.vector.memset(second_plane[h][:].bitcast(I32), 0)
         nc.vector.memset(w4_plane[:].bitcast(I32), 0)
         nc.vector.memset(warm[:, 0:1], 1.0)
         nc.scalar.activation(warm[:, 1:2], warm[:, 0:1], ACT.Sqrt)
@@ -73,39 +72,36 @@ def tile_list_junction_turn_delay_kernel(
             words = wx_words.rearrange("a p c i -> p a (c i)")[:, :, b * PASS * PACK : (b + 1) * PASS * PACK]
             nc.sync.dma_start(out=wx_raw[b][:], in_=words.bitcast(I32))
 
-        nc.sync.dma_start(lists[EXIT][:], offs2)
-        nc.sync.dma_start(lists[ENTRY][:], offs)
-        for r in range(4):
-            nc.scalar.dma_start(
-                out=table_scales[r:P:16, :].bitcast(I32),
-                in_=tab_scales.rearrange("a (q r) c -> r q a c", r=4)[r].bitcast(I32),
-            )
-        for a in range(PASSES):
+        def load_table_scales():
+            for r in range(4):
+                nc.sync.dma_start(
+                    out=table_scales[r:P:16, :].bitcast(I32),
+                    in_=tab_scales.rearrange("a (q r) c -> r q a c", r=4)[r].bitcast(I32),
+                )
+
+        def load_table_words(a):
             nc.sync.dma_start(out=table_words[a][:].bitcast(I32), in_=tab_words[a].bitcast(I32))
-        for q in range(QUADS):
-            nc.gpsimd.dma_start(
-                out=wx_scale_raw[32 * q : 32 * q + 4, :, :].bitcast(I32),
-                in_=wx_scales[:, 4 * q : 4 * q + 4, :].rearrange("a r c -> r a c").bitcast(I32),
-            )
-        nc.gpsimd.dma_start(out=sat_cols[:], in_=sat.rearrange("(b p t) -> p b t", b=PASSES, t=PACK))
-        nc.gpsimd.tensor_scalar(neg_sat[:], sat_cols[:], -1.0, 0.0, ALU.mult, ALU.add)
-        load_wx(0)
-        load_we(0, 0)
-        load_we(0, 1)
-        load_wx(1)
-        load_we(1, 0)
-        load_we(1, 1)
+
+        def load_plane(queue, plane, scales):
+            for q in range(QUADS):
+                queue.dma_start(
+                    out=plane[32 * q : 32 * q + 4].bitcast(I32),
+                    in_=scales[:, 4 * q : 4 * q + 4, :].rearrange("a r c -> r a c").bitcast(I32),
+                )
+
+        def load_columns(queue, cols, vector):
+            queue.dma_start(out=cols[:], in_=vector.rearrange("(b p t) -> p b t", b=PASSES, t=PACK))
 
         picked_words = {}
         first_plane = {}
 
-        def gather_scales(s, h, offset=None):
-            cols = lists[s][:, h * HALF // 16 : (h + 1) * HALF // 16]
-            both = held(f"picked_scales{s}{h}", [P, HALF], U8, offset)
-            nc.vector.tensor_copy(both[:], table_scales[:].indirect(cols))
-            first_plane[s, h] = both
-            queue = nc.scalar if h == 0 else nc.sync
-            queue.dma_start(out=second_plane[s][h][0:100, :].bitcast(I32), in_=both[16:116, :].bitcast(I32))
+        def gather_scales(h, queue, offset=None):
+            both = held(f"picked_scales{h}", [P, 2 * HALF], U8, offset)
+            for s in (EXIT, ENTRY):
+                cols = lists[s][:, h * HALF // 16 : (h + 1) * HALF // 16]
+                nc.vector.tensor_copy(both[:, s * HALF : (s + 1) * HALF], table_scales[:].indirect(cols))
+            first_plane[h] = both
+            queue.dma_start(out=second_plane[h][0:100, :].bitcast(I32), in_=both[16:116, :].bitcast(I32))
 
         def gather_words(s, h, a, offset=None):
             cols = lists[s][:, h * HALF // 16 : (h + 1) * HALF // 16]
@@ -156,61 +152,63 @@ def tile_list_junction_turn_delay_kernel(
                     lhsT=codes[s, b, a][:, cols].bitcast(FP8X4),
                     lhsT_scale=planes[s, b, a][:, cols],
                     rhs=picked_words[s, h, a][:].bitcast(FP4X4),
-                    rhs_scale=(first_plane[s, h] if a == 0 else second_plane[s][h])[:],
+                    rhs_scale=(first_plane if a == 0 else second_plane)[h][:, s * HALF : (s + 1) * HALF],
                     start=(a == 0),
                     stop=(a == PASSES - 1),
                 )
 
         exit_less_sat = {}
 
-        def exit_response(h, b):
-            shifted = held(f"exit_less_sat{h}{b}", [P, PACK, HALF], F32)
-            for t in range(PACK):
-                bank = psum.tile([P, HALF], F32, name="exit_bank", tag="exit_bank", bufs=2)
-                response(EXIT, h, b, t, bank)
-                nc.scalar.activation(shifted[:, t, :], bank[:], ACT.Identity, bias=neg_sat[:, b, t : t + 1])
-            exit_less_sat[h, b] = shifted
+        def exit_response(h, b, t):
+            shifted = held(f"exit_less_sat{h}{b}{t}", [P, HALF], F32, 16384 + 2048 * (8 * h + 4 * b + t))
+            bank = psum.tile([P, HALF], F32, name="exit_bank", tag="exit_bank", bufs=3)
+            response(EXIT, h, b, t, bank)
+            nc.scalar.activation(shifted[:], bank[:], ACT.Identity, bias=neg_sat[:, b, t : t + 1])
+            exit_less_sat[h, b, t] = shifted
 
+        larger = {}
         roots = {}
 
-        def smooth(h, b):
-            larger = work.tile([P, PACK, HALF], F32, name="larger")
-            squared = work.tile([P, PACK, HALF], F32, name="squared")
-            root = work.tile([P, PACK, HALF], F32, name="root")
-            for t in range(PACK):
-                bank = psum.tile([P, HALF], F32, name="entry_bank", tag="entry_bank", bufs=3)
-                response(ENTRY, h, b, t, bank)
-                nc.vector.scalar_tensor_tensor(
-                    larger[:, t, :], bank[:], sat_cols[:, b, t : t + 1], exit_less_sat[h, b][:, t, :],
-                    ALU.subtract, ALU.max,
-                )
-                nc.scalar.activation(squared[:, t, :], larger[:, t, :], ACT.Square)
-                nc.scalar.activation(root[:, t, :], squared[:, t, :], ACT.Sqrt, bias=1.0)
-            roots[h, b] = root
+        def entry_response(h, b, t):
+            if t == 0:
+                larger[h, b] = work.tile([P, PACK, HALF], F32, name="larger", bufs=2)
+                roots[h, b] = held(f"root{h}{b}", [P, PACK, HALF], F32)
+            bank = psum.tile([P, HALF], F32, name="entry_bank", tag="entry_bank", bufs=3)
+            response(ENTRY, h, b, t, bank)
+            nc.vector.scalar_tensor_tensor(
+                larger[h, b][:, t, :], bank[:], sat_cols[:, b, t : t + 1], exit_less_sat[h, b, t][:],
+                ALU.subtract, ALU.max,
+            )
+
+        def smooth_slice(h, b, t):
+            squared = work.tile([P, HALF], F32, name="squared", bufs=3)
+            nc.scalar.activation(squared[:], larger[h, b][:, t, :], ACT.Square)
+            nc.scalar.activation(roots[h, b][:, t, :], squared[:], ACT.Sqrt, bias=1.0)
+
+        def smooth_columns(h, b, c0, width):
+            squared = work.tile([P, PACK, width], F32, name="squared_columns", tag="squared", bufs=3)
+            nc.scalar.activation(squared[:], larger[h, b][:, :, c0 : c0 + width], ACT.Square)
+            nc.scalar.activation(roots[h, b][:, :, c0 : c0 + width], squared[:], ACT.Sqrt, bias=1.0)
 
         h_codes = {}
         h_planes = {}
 
-        def quantize_h(h, b, width):
-            words = held(f"h_codes{h}{b}", [P, HALF], I32)
-            plane = held(f"h_plane{h}{b}", [P, HALF], U8)
-            rounded = held(f"h_rounded{h}{b}", [P, HALF * PACK], BF16)
-            for c0 in range(0, HALF, width):
-                part = rounded[:, c0 * PACK : (c0 + width) * PACK]
-                nc.vector.tensor_tensor(
-                    part.rearrange("p (c j t) -> p c t j", t=PACK, j=4),
-                    roots[h, b][:, :, c0 : c0 + width].rearrange("p t (c j) -> p c t j", j=4),
-                    gain_cols[:, b, :].unsqueeze(1).unsqueeze(3).to_broadcast([P, width // 4, PACK, 4]),
-                    ALU.mult,
-                )
-            for c0 in range(0, HALF, width):
-                nc.vector.quantize_mx(
-                    out=words[:, c0 : c0 + width].bitcast(FP8X4),
-                    scales=plane[:, c0 : c0 + width],
-                    in_=rounded[:, c0 * PACK : (c0 + width) * PACK],
-                )
-            h_codes[h, b] = words
-            h_planes[h, b] = plane
+        def quantize_h(h, b, c0, width):
+            if c0 == 0:
+                h_codes[h, b] = held(f"h_codes{h}{b}", [P, HALF], I32)
+                h_planes[h, b] = held(f"h_plane{h}{b}", [P, HALF], U8)
+            rounded = work.tile([P, width * PACK], BF16, name="rounded", align_bytes=64, bufs=4)
+            nc.vector.tensor_tensor(
+                rounded[:].rearrange("p (c j t) -> p c t j", t=PACK, j=4),
+                roots[h, b][:, :, c0 : c0 + width].rearrange("p t (c j) -> p c t j", j=4),
+                gain_cols[:, b, :].unsqueeze(1).unsqueeze(3).to_broadcast([P, width // 4, PACK, 4]),
+                ALU.mult,
+            )
+            nc.vector.quantize_mx(
+                out=h_codes[h, b][:, c0 : c0 + width].bitcast(FP8X4),
+                scales=h_planes[h, b][:, c0 : c0 + width],
+                in_=rounded[:],
+            )
 
         def project(h, n, c0, width, dest):
             for b in range(PASSES):
@@ -224,67 +222,87 @@ def tile_list_junction_turn_delay_kernel(
                     stop=(b == PASSES - 1),
                 )
 
-        def project_wide(h):
+        def project_wide(h, copy):
             for n in range(N // P):
-                bank = psum.tile([P, HALF], F32, name="out_bank", tag="out_bank", bufs=3)
+                bank = psum.tile([P, HALF], F32, name="out_bank", tag="out_bank", bufs=2)
                 project(h, n, 0, HALF, bank[:])
                 staged = held(f"staged{h}{n}", [P, HALF], F32)
-                nc.scalar.copy(staged[:], bank[:])
+                copy(staged[:], bank[:])
                 nc.sync.dma_start(out=out[n * P : (n + 1) * P, h * HALF : (h + 1) * HALF], in_=staged[:])
 
-        def project_narrow(h):
-            for c0 in range(0, HALF, CHUNK):
-                bank = psum.tile([P, N // P, CHUNK], F32, name="out_bank_narrow", tag="out_bank", bufs=3)
-                for n in range(N // P):
-                    project(h, n, c0, CHUNK, bank[:, n, :])
-                staged = held(f"staged_narrow{c0}", [P, N // P, CHUNK], F32)
-                nc.scalar.copy(staged[:], bank[:])
-                cols = out[:, h * HALF + c0 : h * HALF + c0 + CHUNK]
-                nc.sync.dma_start(out=cols.rearrange("(n p) c -> p n c", p=P), in_=staged[:])
+        def project_narrow(h, c0, copy):
+            bank = psum.tile([P, N // P, CHUNK], F32, name="out_bank_narrow", tag="out_bank", bufs=2)
+            for n in range(N // P):
+                project(h, n, c0, CHUNK, bank[:, n, :])
+            staged = held(f"staged_narrow{h}{c0}", [P, N // P, CHUNK], F32)
+            copy(staged[:], bank[:])
+            cols = out[:, h * HALF + c0 : h * HALF + c0 + CHUNK]
+            nc.sync.dma_start(out=cols.rearrange("(n p) c -> p n c", p=P), in_=staged[:])
 
-        gather_scales(EXIT, 0)
-        gather_scales(ENTRY, 0)
+        nc.sync.dma_start(lists[EXIT][:], offs2)
+        nc.sync.dma_start(lists[ENTRY][:], offs)
+        load_table_words(0)
+        load_table_scales()
+        load_table_words(1)
+        gather_scales(0, nc.scalar)
+        load_we(0, 0)
+        load_wx(0)
+        load_plane(nc.sync, wx_scale_raw, wx_scales)
+        load_we(0, 1)
+        load_wx(1)
+        load_we(1, 0)
+        load_we(1, 1)
+        load_columns(nc.gpsimd, sat_cols, sat)
+        nc.gpsimd.tensor_scalar(neg_sat[:], sat_cols[:], -1.0, 0.0, ALU.mult, ALU.add)
+        load_columns(nc.gpsimd, gain_cols, gain)
+        nc.gpsimd.dma_start(
+            out=w4_codes[:].rearrange("p (a c) -> p a c", a=PASSES).bitcast(I32),
+            in_=w4_words.rearrange("a p c -> p a c").bitcast(I32),
+        )
+        load_plane(nc.gpsimd, w4_plane[:].rearrange("p (a c) -> p a c", a=PASSES), w4_scales)
         gather_words(EXIT, 0, 0)
         gather_words(ENTRY, 0, 0)
         gather_words(EXIT, 0, 1)
         order_wx(0)
         gather_words(ENTRY, 0, 1)
-        exit_response(0, 0)
         round_we(0, 0, nc.scalar.copy)
         round_we(0, 1, nc.vector.tensor_copy)
         quantize_we(0, 0)
         quantize_we(0, 1)
-        nc.gpsimd.dma_start(out=gain_cols[:], in_=gain.rearrange("(b p t) -> p b t", b=PASSES, t=PACK))
-        nc.gpsimd.dma_start(
-            out=w4_codes[:].rearrange("p (a c) -> p a c", a=PASSES).bitcast(I32),
-            in_=w4_words.rearrange("a p c -> p a c").bitcast(I32),
-        )
-        for q in range(QUADS):
-            nc.gpsimd.dma_start(
-                out=w4_plane[32 * q : 32 * q + 4, :].rearrange("p (a c) -> p a c", a=PASSES).bitcast(I32),
-                in_=w4_scales[:, 4 * q : 4 * q + 4, :].rearrange("a r c -> r a c").bitcast(I32),
-            )
+        for t in range(PACK):
+            exit_response(0, 0, t)
         order_wx(1)
-        smooth(0, 0)
-        gather_scales(EXIT, 1, 4096 + 2048)
-        gather_words(EXIT, 1, 0, 4096)
-        gather_words(EXIT, 1, 1, 4096 + 1024)
-        exit_response(0, 1)
         round_we(1, 0, nc.scalar.copy)
         round_we(1, 1, nc.vector.tensor_copy)
         quantize_we(1, 0)
         quantize_we(1, 1)
-        gather_scales(ENTRY, 1, 3 * 4096 + 2048)
-        gather_words(ENTRY, 1, 0, 3 * 4096)
-        gather_words(ENTRY, 1, 1, 3 * 4096 + 1024)
-        smooth(0, 1)
-        quantize_h(0, 0, 512)
-        exit_response(1, 0)
-        smooth(1, 0)
-        quantize_h(0, 1, 512)
-        project_wide(0)
-        exit_response(1, 1)
-        smooth(1, 1)
-        quantize_h(1, 0, 512)
-        quantize_h(1, 1, CHUNK)
-        project_narrow(1)
+        for t in range(PACK):
+            entry_response(0, 0, t)
+            smooth_slice(0, 0, t)
+            exit_response(0, 1, t)
+        gather_scales(1, nc.sync, 16384)
+        gather_words(EXIT, 1, 0, 12288)
+        gather_words(EXIT, 1, 1, 13312)
+        for t in range(PACK):
+            entry_response(0, 1, t)
+            smooth_slice(0, 1, t)
+            exit_response(1, 0, t)
+        gather_words(ENTRY, 1, 0, 24576)
+        gather_words(ENTRY, 1, 1, 26624)
+        for c0 in range(0, HALF, 256):
+            quantize_h(0, 0, c0, 256)
+        for t in range(PACK):
+            entry_response(1, 0, t)
+            smooth_slice(1, 0, t)
+            exit_response(1, 1, t)
+        for t in range(PACK):
+            entry_response(1, 1, t)
+        for c0 in range(0, HALF, 256):
+            quantize_h(0, 1, c0, 256)
+        project_wide(0, nc.scalar.copy)
+        for c0 in range(0, HALF, 256):
+            quantize_h(1, 0, c0, 256)
+        for c0 in range(0, HALF, CHUNK):
+            smooth_columns(1, 1, c0, CHUNK)
+            quantize_h(1, 1, c0, CHUNK)
+            project_narrow(1, c0, nc.scalar.copy)

@@ -44,19 +44,18 @@ def tile_list_junction_turn_delay_kernel(
         lists = [held("entry_list", [P, S // 16], U16), held("exit_list", [P, S // 16], U16)]
         table_scales = held("table_scales", [P, T], U8)
         table_words = [held(f"table_words{a}", [P, T], U16) for a in range(PASSES)]
-        wx_raw = [held(f"wx_raw{b}", [P, PASSES, PASS], I32) for b in range(PASSES)]
-        wx_scale_raw = held("wx_scale_raw", [P, PASSES, H], U8)
-        we_raw = [[held(f"we_raw{b}{a}", [P, PACK, PASS], F32) for a in range(PASSES)] for b in range(PASSES)]
+        wx_raw = {}
+        wx_scale_raw = held("wx_scale_raw", [P, PASSES, H], U8, 49152 + 20480 + 64)
+        we_raw = {}
         w4_codes = held("w4_codes", [P, PASSES * 2 * N], U8)
         w4_plane = held("w4_plane", [P, PASSES * N], U8)
         sat_cols = held("sat_cols", [P, PASSES, PACK], F32)
-        neg_sat = held("neg_sat", [P, PASSES, PACK], F32)
         gain_cols = held("gain_cols", [P, PASSES, PACK], F32)
         second_plane = [held(f"second_plane{h}", [P, 2 * HALF], U8) for h in range(HALVES)]
         warm = held("warm", [P, 2], F32)
 
-        nc.vector.memset(table_scales[:, : 3 * T // 4].bitcast(I32), 0)
-        nc.gpsimd.memset(table_scales[:, 3 * T // 4 :].bitcast(I32), 0)
+        nc.vector.memset(table_scales[:, : T // 2].bitcast(I32), 0)
+        nc.gpsimd.memset(table_scales[:, T // 2 :].bitcast(I32), 0)
         nc.vector.memset(wx_scale_raw[:].bitcast(I32), 0)
         for h in range(HALVES):
             nc.vector.memset(second_plane[h][:].bitcast(I32), 0)
@@ -66,10 +65,12 @@ def tile_list_junction_turn_delay_kernel(
 
         def load_we(b, a):
             rows = we[a * PASS : (a + 1) * PASS, b * PASS : (b + 1) * PASS]
-            nc.sync.dma_start(out=we_raw[b][a][:], in_=rows.rearrange("(p i) c -> p i c", i=PACK))
+            we_raw[b, a] = held(f"we_raw{b}{a}", [P, PACK, PASS], F32, 49152 + 8192 * a + 64 * min(a + b, 1))
+            nc.sync.dma_start(out=we_raw[b, a][:], in_=rows.rearrange("(p i) c -> p i c", i=PACK))
 
         def load_wx(b):
             words = wx_words.rearrange("a p c i -> p a (c i)")[:, :, b * PASS * PACK : (b + 1) * PASS * PACK]
+            wx_raw[b] = held(f"wx_raw{b}", [P, PASSES, PASS], I32, 49152 + 16384 + 64 - 2048 + 2048 * b)
             nc.sync.dma_start(out=wx_raw[b][:], in_=words.bitcast(I32))
 
         def load_table_scales():
@@ -133,7 +134,7 @@ def tile_list_junction_turn_delay_kernel(
             rounded = held(f"we_rounded{b}{a}", [P, PASS * PACK], BF16, 4096 * (2 * b + a))
             copy(
                 rounded[:].rearrange("p (t m i) -> p m i t", t=PACK, i=PACK),
-                we_raw[b][a][:].rearrange("p i (m t) -> p m i t", t=PACK),
+                we_raw[b, a][:].rearrange("p i (m t) -> p m i t", t=PACK),
             )
             rounded_we[b, a] = rounded
 
@@ -210,30 +211,33 @@ def tile_list_junction_turn_delay_kernel(
                 in_=rounded[:],
             )
 
-        def project(h, n, c0, width, dest):
-            for b in range(PASSES):
-                nc.tensor.matmul_mx(
-                    out=dest,
-                    lhsT=w4_codes[:, 2 * (b * N + n * P) : 2 * (b * N + (n + 1) * P)].bitcast(FP4X4),
-                    lhsT_scale=w4_plane[:, b * N + n * P : b * N + (n + 1) * P],
-                    rhs=h_codes[h, b][:, c0 : c0 + width].bitcast(FP8X4),
-                    rhs_scale=h_planes[h, b][:, c0 : c0 + width],
-                    start=(b == 0),
-                    stop=(b == PASSES - 1),
-                )
+        def project(h, n, b, c0, width, dest, start, stop):
+            nc.tensor.matmul_mx(
+                out=dest,
+                lhsT=w4_codes[:, 2 * (b * N + n * P) : 2 * (b * N + (n + 1) * P)].bitcast(FP4X4),
+                lhsT_scale=w4_plane[:, b * N + n * P : b * N + (n + 1) * P],
+                rhs=h_codes[h, b][:, c0 : c0 + width].bitcast(FP8X4),
+                rhs_scale=h_planes[h, b][:, c0 : c0 + width],
+                start=start,
+                stop=stop,
+            )
 
         def project_wide(h, copy):
             for n in range(N // P):
                 bank = psum.tile([P, HALF], F32, name="out_bank", tag="out_bank", bufs=2)
-                project(h, n, 0, HALF, bank[:])
+                for b in range(PASSES):
+                    project(h, n, b, 0, HALF, bank[:], b == 0, b == PASSES - 1)
                 staged = held(f"staged{h}{n}", [P, HALF], F32)
                 copy(staged[:], bank[:])
                 nc.sync.dma_start(out=out[n * P : (n + 1) * P, h * HALF : (h + 1) * HALF], in_=staged[:])
 
         def project_narrow(h, c0, copy):
-            bank = psum.tile([P, N // P, CHUNK], F32, name="out_bank_narrow", tag="out_bank", bufs=2)
-            for n in range(N // P):
-                project(h, n, c0, CHUNK, bank[:, n, :])
+            tag = "exit_bank" if c0 < CHUNK else "entry_bank"
+            bank = psum.tile([P, N // P, CHUNK], F32, name="out_bank_narrow", tag=tag, bufs=3)
+            for b in range(PASSES):
+                for n in range(N // P):
+                    first, last = (b, n) == (0, 0), (b, n) == (PASSES - 1, N // P - 1)
+                    project(h, n, b, c0, CHUNK, bank[:, n, :], first, last)
             staged = held(f"staged_narrow{h}{c0}", [P, N // P, CHUNK], F32)
             copy(staged[:], bank[:])
             cols = out[:, h * HALF + c0 : h * HALF + c0 + CHUNK]
@@ -243,35 +247,36 @@ def tile_list_junction_turn_delay_kernel(
         nc.sync.dma_start(lists[ENTRY][:], offs)
         load_table_words(0)
         load_table_scales()
+        load_columns(nc.sync, sat_cols, sat)
         load_table_words(1)
-        gather_scales(0, nc.scalar)
-        load_we(0, 0)
         load_wx(0)
         load_plane(nc.sync, wx_scale_raw, wx_scales)
-        load_we(0, 1)
-        load_wx(1)
-        load_we(1, 0)
-        load_we(1, 1)
-        load_columns(nc.gpsimd, sat_cols, sat)
-        nc.gpsimd.tensor_scalar(neg_sat[:], sat_cols[:], -1.0, 0.0, ALU.mult, ALU.add)
-        load_columns(nc.gpsimd, gain_cols, gain)
+        gather_words(EXIT, 0, 0)
+        gather_scales(0, nc.scalar)
+        load_we(0, 0)
+        load_columns(nc.sync, gain_cols, gain)
         nc.gpsimd.dma_start(
             out=w4_codes[:].rearrange("p (a c) -> p a c", a=PASSES).bitcast(I32),
             in_=w4_words.rearrange("a p c -> p a c").bitcast(I32),
         )
         load_plane(nc.gpsimd, w4_plane[:].rearrange("p (a c) -> p a c", a=PASSES), w4_scales)
-        gather_words(EXIT, 0, 0)
-        gather_words(ENTRY, 0, 0)
         gather_words(EXIT, 0, 1)
         order_wx(0)
-        gather_words(ENTRY, 0, 1)
+        load_we(0, 1)
+        load_wx(1)
         round_we(0, 0, nc.scalar.copy)
-        round_we(0, 1, nc.vector.tensor_copy)
+        neg_sat = held("neg_sat", [P, PASSES, PACK], F32, 49152)
+        nc.scalar.activation(neg_sat[:], sat_cols[:], ACT.Copy, scale=-1.0)
+        order_wx(1)
+        gather_words(ENTRY, 0, 0, 49152 + 20480 + 64)
+        gather_words(ENTRY, 0, 1, 49152 + 21504 + 64)
+        round_we(0, 1, nc.scalar.copy)
         quantize_we(0, 0)
         quantize_we(0, 1)
         for t in range(PACK):
             exit_response(0, 0, t)
-        order_wx(1)
+        load_we(1, 0)
+        load_we(1, 1)
         round_we(1, 0, nc.scalar.copy)
         round_we(1, 1, nc.vector.tensor_copy)
         quantize_we(1, 0)
@@ -280,9 +285,9 @@ def tile_list_junction_turn_delay_kernel(
             entry_response(0, 0, t)
             smooth_slice(0, 0, t)
             exit_response(0, 1, t)
-        gather_scales(1, nc.sync, 16384)
-        gather_words(EXIT, 1, 0, 12288)
-        gather_words(EXIT, 1, 1, 13312)
+        gather_scales(1, nc.sync, 0)
+        gather_words(EXIT, 1, 0, 1024)
+        gather_words(EXIT, 1, 1, 18432)
         for t in range(PACK):
             entry_response(0, 1, t)
             smooth_slice(0, 1, t)
@@ -299,10 +304,11 @@ def tile_list_junction_turn_delay_kernel(
             entry_response(1, 1, t)
         for c0 in range(0, HALF, 256):
             quantize_h(0, 1, c0, 256)
-        project_wide(0, nc.scalar.copy)
         for c0 in range(0, HALF, 256):
             quantize_h(1, 0, c0, 256)
         for c0 in range(0, HALF, CHUNK):
             smooth_columns(1, 1, c0, CHUNK)
+        project_wide(0, nc.scalar.copy)
+        for c0 in range(0, HALF, CHUNK):
             quantize_h(1, 1, c0, CHUNK)
             project_narrow(1, c0, nc.scalar.copy)

from contextlib import ExitStack

import concourse.mybir as mybir

K, H, N, T, S = 1024, 1024, 384, 4096, 1024
FLOPS = 2 * (2 * K * H * S + H * N * S)

F32 = mybir.dt.float32
BF16 = mybir.dt.bfloat16
I32 = mybir.dt.int32
U16 = mybir.dt.uint16
U8 = mybir.dt.uint8
FP8X4 = mybir.dt.float8_e4m3fn_x4
FP4X4 = mybir.dt.float4_e2m1fn_x4
ALU = mybir.AluOpType
ACT = mybir.ActivationFunctionType

P = 128
PACK = 4
PASS = P * PACK
PASSES = 2
HALF = 512
HALVES = S // HALF
QUADS = 4
ENTRY, EXIT = 0, 1
CHUNK = 128


def tile_list_junction_turn_delay_kernel(
    tc, tab_words, tab_scales, offs, offs2, we, wx_words, wx_scales, sat, gain, w4_words, w4_scales, out
):
    nc = tc.nc
    with ExitStack() as ctx:
        keep = ctx.enter_context(tc.tile_pool(name="keep", bufs=1))
        work = ctx.enter_context(tc.tile_pool(name="work", bufs=2))
        shared = ctx.enter_context(tc.tile_pool(name="shared", bufs=1))
        psum = ctx.enter_context(tc.psum_pool(name="psum", bufs=1))

        def held(name, shape, dtype, offset=None):
            if offset is None:
                return keep.tile(shape, dtype, name=name, align_bytes=64)
            return shared.tile(shape, dtype, name=name, align_bytes=64, offset=offset)

        lists = [held("entry_list", [P, S // 16], U16), held("exit_list", [P, S // 16], U16)]
        table_scales = held("table_scales", [P, T], U8)
        table_words = [held(f"table_words{a}", [P, T], U16) for a in range(PASSES)]
        wx_raw = {}
        wx_scale_raw = held("wx_scale_raw", [P, PASSES, H], U8, 49152 + 20480 + 64)
        we_raw = {}
        w4_codes = held("w4_codes", [P, PASSES * 2 * N], U8)
        w4_plane = held("w4_plane", [P, PASSES * N], U8)
        sat_cols = held("sat_cols", [P, PASSES, PACK], F32)
        gain_cols = held("gain_cols", [P, PASSES, PACK], F32)
        second_plane = [held(f"second_plane{h}", [P, 2 * HALF], U8) for h in range(HALVES)]
        warm = held("warm", [P, 2], F32)

        nc.vector.memset(table_scales[:, : T // 2].bitcast(I32), 0)
        nc.gpsimd.memset(table_scales[:, T // 2 :].bitcast(I32), 0)
        nc.vector.memset(wx_scale_raw[:].bitcast(I32), 0)
        for h in range(HALVES):
            nc.vector.memset(second_plane[h][:].bitcast(I32), 0)
        nc.vector.memset(w4_plane[:].bitcast(I32), 0)
        nc.vector.memset(warm[:, 0:1], 1.0)
        nc.scalar.activation(warm[:, 1:2], warm[:, 0:1], ACT.Sqrt)

        def load_we(b, a):
            rows = we[a * PASS : (a + 1) * PASS, b * PASS : (b + 1) * PASS]
            we_raw[b, a] = held(f"we_raw{b}{a}", [P, PACK, PASS], F32, 49152 + 8192 * a + 64 * min(a + b, 1))
            nc.sync.dma_start(out=we_raw[b, a][:], in_=rows.rearrange("(p i) c -> p i c", i=PACK))

        def load_wx(b):
            words = wx_words.rearrange("a p c i -> p a (c i)")[:, :, b * PASS * PACK : (b + 1) * PASS * PACK]
            wx_raw[b] = held(f"wx_raw{b}", [P, PASSES, PASS], I32, 49152 + 16384 + 64 - 2048 + 2048 * b)
            nc.sync.dma_start(out=wx_raw[b][:], in_=words.bitcast(I32))

        def load_table_scales():
            for r in range(4):
                nc.sync.dma_start(
                    out=table_scales[r:P:16, :].bitcast(I32),
                    in_=tab_scales.rearrange("a (q r) c -> r q a c", r=4)[r].bitcast(I32),
                )

        def load_table_words(a):
            nc.sync.dma_start(out=table_words[a][:].bitcast(I32), in_=tab_words[a].bitcast(I32))

        def load_plane(queue, plane, scales):
            for q in range(QUADS):
                queue.dma_start(
                    out=plane[32 * q : 32 * q + 4].bitcast(I32),
                    in_=scales[:, 4 * q : 4 * q + 4, :].rearrange("a r c -> r a c").bitcast(I32),
                )

        def load_columns(queue, cols, vector):
            queue.dma_start(out=cols[:], in_=vector.rearrange("(b p t) -> p b t", b=PASSES, t=PACK))

        picked_words = {}
        first_plane = {}

        def gather_scales(h, queue, offset=None):
            both = held(f"picked_scales{h}", [P, 2 * HALF], U8, offset)
            for s in (EXIT, ENTRY):
                cols = lists[s][:, h * HALF // 16 : (h + 1) * HALF // 16]
                nc.vector.tensor_copy(both[:, s * HALF : (s + 1) * HALF], table_scales[:].indirect(cols))
            first_plane[h] = both
            queue.dma_start(out=second_plane[h][0:100, :].bitcast(I32), in_=both[16:116, :].bitcast(I32))

        def gather_words(s, h, a, offset=None):
            cols = lists[s][:, h * HALF // 16 : (h + 1) * HALF // 16]
            words = held(f"picked_words{s}{h}{a}", [P, HALF], U16, offset)
            nc.vector.tensor_copy(words[:], table_words[a][:].indirect(cols))
            picked_words[s, h, a] = words

        codes = {}
        planes = {}

        def order_wx(b):
            words = held(f"wx_codes{b}", [P, PASSES, PASS], I32)
            nc.vector.tensor_copy(
                words[:].rearrange("p a (t g m) -> p a g t m", t=PACK, m=4),
                wx_raw[b][:].rearrange("p a (g m t) -> p a g t m", t=PACK, m=4),
            )
            plane = held(f"wx_plane{b}", [P, PASSES, PASS], U8)
            nc.vector.tensor_copy(
                plane[:].rearrange("p a (t m) -> p a t m", t=PACK),
                wx_scale_raw[:, :, b * PASS : (b + 1) * PASS].rearrange("p a (m t) -> p a t m", t=PACK),
            )
            for a in range(PASSES):
                codes[EXIT, b, a] = words[:, a, :]
                planes[EXIT, b, a] = plane[:, a, :]

        rounded_we = {}

        def round_we(b, a, copy):
            rounded = held(f"we_rounded{b}{a}", [P, PASS * PACK], BF16, 4096 * (2 * b + a))
            copy(
                rounded[:].rearrange("p (t m i) -> p m i t", t=PACK, i=PACK),
                we_raw[b, a][:].rearrange("p i (m t) -> p m i t", t=PACK),
            )
            rounded_we[b, a] = rounded

        def quantize_we(b, a):
            words = held(f"we_codes{b}{a}", [P, PASS], I32)
            plane = held(f"we_plane{b}{a}", [P, PASS], U8)
            nc.vector.quantize_mx(out=words[:].bitcast(FP8X4), scales=plane[:], in_=rounded_we[b, a][:])
            codes[ENTRY, b, a] = words[:]
            planes[ENTRY, b, a] = plane[:]

        def response(s, h, b, t, bank):
            cols = slice(t * P, (t + 1) * P)
            for a in range(PASSES):
                nc.tensor.matmul_mx(
                    out=bank[:],
                    lhsT=codes[s, b, a][:, cols].bitcast(FP8X4),
                    lhsT_scale=planes[s, b, a][:, cols],
                    rhs=picked_words[s, h, a][:].bitcast(FP4X4),
                    rhs_scale=(first_plane if a == 0 else second_plane)[h][:, s * HALF : (s + 1) * HALF],
                    start=(a == 0),
                    stop=(a == PASSES - 1),
                )

        exit_less_sat = {}

        def exit_response(h, b, t):
            shifted = held(f"exit_less_sat{h}{b}{t}", [P, HALF], F32, 16384 + 2048 * (8 * h + 4 * b + t))
            bank = psum.tile([P, HALF], F32, name="exit_bank", tag="exit_bank", bufs=3)
            response(EXIT, h, b, t, bank)
            nc.scalar.activation(shifted[:], bank[:], ACT.Identity, bias=neg_sat[:, b, t : t + 1])
            exit_less_sat[h, b, t] = shifted

        larger = {}
        roots = {}

        def entry_response(h, b, t):
            if t == 0:
                larger[h, b] = work.tile([P, PACK, HALF], F32, name="larger", bufs=2)
                roots[h, b] = held(f"root{h}{b}", [P, PACK, HALF], F32)
            bank = psum.tile([P, HALF], F32, name="entry_bank", tag="entry_bank", bufs=3)
            response(ENTRY, h, b, t, bank)
            nc.vector.scalar_tensor_tensor(
                larger[h, b][:, t, :], bank[:], sat_cols[:, b, t : t + 1], exit_less_sat[h, b, t][:],
                ALU.subtract, ALU.max,
            )

        def smooth_slice(h, b, t):
            squared = work.tile([P, HALF], F32, name="squared", bufs=3)
            nc.scalar.activation(squared[:], larger[h, b][:, t, :], ACT.Square)
            nc.scalar.activation(roots[h, b][:, t, :], squared[:], ACT.Sqrt, bias=1.0)

        def smooth_columns(h, b, c0, width):
            squared = work.tile([P, PACK, width], F32, name="squared_columns", tag="squared", bufs=3)
            nc.scalar.activation(squared[:], larger[h, b][:, :, c0 : c0 + width], ACT.Square)
            nc.scalar.activation(roots[h, b][:, :, c0 : c0 + width], squared[:], ACT.Sqrt, bias=1.0)

        h_codes = {}
        h_planes = {}

        def quantize_h(h, b, c0, width):
            if c0 == 0:
                h_codes[h, b] = held(f"h_codes{h}{b}", [P, HALF], I32)
                h_planes[h, b] = held(f"h_plane{h}{b}", [P, HALF], U8)
            rounded = work.tile([P, width * PACK], BF16, name="rounded", align_bytes=64, bufs=4)
            nc.vector.tensor_tensor(
                rounded[:].rearrange("p (c j t) -> p c t j", t=PACK, j=4),
                roots[h, b][:, :, c0 : c0 + width].rearrange("p t (c j) -> p c t j", j=4),
                gain_cols[:, b, :].unsqueeze(1).unsqueeze(3).to_broadcast([P, width // 4, PACK, 4]),
                ALU.mult,
            )
            nc.vector.quantize_mx(
                out=h_codes[h, b][:, c0 : c0 + width].bitcast(FP8X4),
                scales=h_planes[h, b][:, c0 : c0 + width],
                in_=rounded[:],
            )

        def project(h, n, b, c0, width, dest, start, stop):
            nc.tensor.matmul_mx(
                out=dest,
                lhsT=w4_codes[:, 2 * (b * N + n * P) : 2 * (b * N + (n + 1) * P)].bitcast(FP4X4),
                lhsT_scale=w4_plane[:, b * N + n * P : b * N + (n + 1) * P],
                rhs=h_codes[h, b][:, c0 : c0 + width].bitcast(FP8X4),
                rhs_scale=h_planes[h, b][:, c0 : c0 + width],
                start=start,
                stop=stop,
            )

        def project_wide(h, copy):
            for n in range(N // P):
                bank = psum.tile([P, HALF], F32, name="out_bank", tag="out_bank", bufs=2)
                for b in range(PASSES):
                    project(h, n, b, 0, HALF, bank[:], b == 0, b == PASSES - 1)
                staged = held(f"staged{h}{n}", [P, HALF], F32)
                copy(staged[:], bank[:])
                nc.sync.dma_start(out=out[n * P : (n + 1) * P, h * HALF : (h + 1) * HALF], in_=staged[:])

        def project_narrow(h, c0, copy):
            tag = "exit_bank" if c0 < CHUNK else "entry_bank"
            bank = psum.tile([P, N // P, CHUNK], F32, name="out_bank_narrow", tag=tag, bufs=3)
            for b in range(PASSES):
                for n in range(N // P):
                    first, last = (b, n) == (0, 0), (b, n) == (PASSES - 1, N // P - 1)
                    project(h, n, b, c0, CHUNK, bank[:, n, :], first, last)
            staged = held(f"staged_narrow{h}{c0}", [P, N // P, CHUNK], F32)
            copy(staged[:], bank[:])
            cols = out[:, h * HALF + c0 : h * HALF + c0 + CHUNK]
            nc.sync.dma_start(out=cols.rearrange("(n p) c -> p n c", p=P), in_=staged[:])

        nc.sync.dma_start(lists[EXIT][:], offs2)
        nc.sync.dma_start(lists[ENTRY][:], offs)
        load_table_words(0)
        load_table_scales()
        load_columns(nc.sync, sat_cols, sat)
        load_table_words(1)
        load_wx(0)
        load_plane(nc.sync, wx_scale_raw, wx_scales)
        gather_words(EXIT, 0, 0)
        gather_scales(0, nc.scalar)
        load_we(0, 0)
        load_columns(nc.sync, gain_cols, gain)
        nc.gpsimd.dma_start(
            out=w4_codes[:].rearrange("p (a c) -> p a c", a=PASSES).bitcast(I32),
            in_=w4_words.rearrange("a p c -> p a c").bitcast(I32),
        )
        load_plane(nc.gpsimd, w4_plane[:].rearrange("p (a c) -> p a c", a=PASSES), w4_scales)
        gather_words(EXIT, 0, 1)
        order_wx(0)
        load_we(0, 1)
        load_wx(1)
        round_we(0, 0, nc.scalar.copy)
        neg_sat = held("neg_sat", [P, PASSES, PACK], F32, 49152)
        nc.scalar.activation(neg_sat[:], sat_cols[:], ACT.Copy, scale=-1.0)
        order_wx(1)
        gather_words(ENTRY, 0, 0, 49152 + 20480 + 64)
        gather_words(ENTRY, 0, 1, 49152 + 21504 + 64)
        round_we(0, 1, nc.scalar.copy)
        quantize_we(0, 0)
        quantize_we(0, 1)
        for t in range(PACK):
            exit_response(0, 0, t)
        load_we(1, 0)
        load_we(1, 1)
        round_we(1, 0, nc.scalar.copy)
        round_we(1, 1, nc.vector.tensor_copy)
        quantize_we(1, 0)
        quantize_we(1, 1)
        for t in range(PACK):
            entry_response(0, 0, t)
            smooth_slice(0, 0, t)
            exit_response(0, 1, t)
        gather_scales(1, nc.sync, 0)
        gather_words(EXIT, 1, 0, 1024)
        gather_words(EXIT, 1, 1, 18432)
        for t in range(PACK):
            entry_response(0, 1, t)
            smooth_slice(0, 1, t)
            exit_response(1, 0, t)
        gather_words(ENTRY, 1, 0, 24576)
        gather_words(ENTRY, 1, 1, 26624)
        for c0 in range(0, HALF, 256):
            quantize_h(0, 0, c0, 256)
        for t in range(PACK):
            entry_response(1, 0, t)
            smooth_slice(1, 0, t)
            exit_response(1, 1, t)
        for t in range(PACK):
            entry_response(1, 1, t)
        for c0 in range(0, HALF, 256):
            quantize_h(0, 1, c0, 256)
        for c0 in range(0, HALF, 256):
            quantize_h(1, 0, c0, 256)
        for c0 in range(0, HALF, CHUNK):
            smooth_columns(1, 1, c0, CHUNK)
        project_wide(0, nc.scalar.copy)
        for c0 in range(0, HALF, CHUNK):
            quantize_h(1, 1, c0, CHUNK)
            project_narrow(1, c0, nc.scalar.copy)
